import numpy as np
import ml_dtypes


def mxq(x, axis, fmt="e4m3"):
    dtype, down = {"e4m3": (ml_dtypes.float8_e4m3fn, 7), "e5m2": (ml_dtypes.float8_e5m2, 14)}[fmt]
    v = np.moveaxis(np.asarray(x, np.float32).astype(ml_dtypes.bfloat16).astype(np.float64), axis, -1)
    blocks = v.reshape(v.shape[:-1] + (-1, 32))
    amax = np.abs(blocks).max(-1, keepdims=True)
    byte = np.maximum(np.where(amax > 0, np.frexp(amax)[1] - 1 + 127, 0) - down, 1)
    scale = np.exp2(byte - 127.0)
    codes = (blocks / scale).astype(np.float32).astype(dtype).astype(np.float64)
    return np.moveaxis((codes * scale).reshape(v.shape), -1, axis)


WIDE = False


def mx_kscale(k):
    if not WIDE:
        return np.ones(k)
    levels = np.array([10, -10, 5, -5, 0])
    if k % 512:
        return np.exp2(np.random.permutation(np.resize(levels, k // 32))).repeat(32)
    a = np.empty((k // 512, 16))
    for p in range(k // 512):
        a[p, :8] = np.random.permutation(np.resize(levels, 8))
        for g in range(8):
            far = levels[np.abs(levels - a[p, g]) >= 10]
            a[p, g + 8] = far[np.random.randint(len(far))]
    return np.exp2(a.ravel()).repeat(32)


def f64(x):
    return np.asarray(x).astype(np.float64)


def striped(idx):
    return np.tile(np.asarray(idx).reshape(-1, 16).T, (8, 1)).astype(np.uint16)


def unstriped(offs):
    return offs[:16].T.reshape(-1).astype(np.int64)


E2M1 = np.array([0.0, 0.5, 1.0, 1.5, 2.0, 3.0, 4.0, 6.0, -0.0, -0.5, -1.0, -1.5, -2.0, -3.0, -4.0, -6.0])


def pack_weight(w, fmt):
    k, n = w.shape
    w = f64(np.asarray(w, np.float32).astype(ml_dtypes.bfloat16)).reshape(k // 32, 32, n)
    amax = np.abs(w).max(1)
    if fmt == "e4m3":
        byte = np.frexp(amax)[1] - 1 + 127 - 7
    else:
        mant, ex = np.frexp(amax / 6.0)
        byte = np.where(mant > 0.5, ex, ex - 1) + 127
    byte = np.clip(np.where(amax > 0, byte, 1), 1, 254)
    scaled = (w * np.exp2(127.0 - byte)[:, None, :]).reshape(k, n).astype(np.float32)
    by_word = np.ascontiguousarray(scaled.reshape(k // 512, 128, 4, n).transpose(0, 1, 3, 2))
    if fmt == "e4m3":
        words = by_word.astype(ml_dtypes.float8_e4m3fn).view(np.uint8)
    else:
        c = by_word.astype(ml_dtypes.float4_e2m1fn).view(np.uint8) & 0xF
        words = (c[..., 0::2] | (c[..., 1::2] << 4)).reshape(k // 512, 128, 2 * n)
    return np.ascontiguousarray(words), np.ascontiguousarray(byte.astype(np.uint8).reshape(k // 512, 16, n))


def unpack_weight(words, scales, fmt):
    g, _, n = scales.shape
    words = np.ascontiguousarray(words).reshape(g, 128, n, -1)
    if fmt == "e4m3":
        vals = words.view(ml_dtypes.float8_e4m3fn).astype(np.float64)
    else:
        nib = np.empty((g, 128, n, 4), np.uint8)
        nib[..., 0::2] = words & 0xF
        nib[..., 1::2] = words >> 4
        vals = E2M1[nib]
    vals = vals * np.repeat(np.exp2(scales.astype(np.float64) - 127.0), 8, axis=1)[..., None]
    return vals.transpose(0, 1, 3, 2).reshape(g * 512, n)


def bf(x):
    return np.asarray(x, np.float32).astype(ml_dtypes.bfloat16)


def planes(Y):
    r, m = Y.shape
    b = f64(bf(Y)).reshape(r // 32, 32, m)
    amax = np.abs(b).max(1)
    byte = np.clip(np.where(amax > 0, np.frexp(amax)[1] - 1 + 127 - 7, 1), 1, 254)
    codes = (b * np.exp2(127.0 - byte)[:, None, :]).reshape(r, m).astype(np.float32).astype(ml_dtypes.float8_e4m3fn).view(np.uint8)
    words = codes.reshape(r // 512, 128, 4, m).transpose(0, 1, 3, 2)
    return np.ascontiguousarray(words), np.ascontiguousarray(byte.astype(np.uint8).reshape(r // 512, 16, m))


D, T, I, J, U, H, M = 512, 2048, 512, 512, 1024, 512, 1024


def setup_inputs():
    n = np.random.standard_normal
    idx = np.random.permutation(T)[:I]
    idx2 = np.random.permutation(U)[:J]
    idx3 = np.random.permutation(M)[:J]
    fd = mx_kscale(D)
    fh = mx_kscale(H)
    keysp = pack_weight(n((D, T)) / fd[:, None], "e2m1")
    return {
        "keys_words": keysp[0],
        "keys_scales": keysp[1],
        "wk": (n((D, H)) * 1.0 / np.sqrt(D) * fd[:, None] * fh).astype(np.float32),
        "notes": (n((H, U)) * 1.0 / np.sqrt(H) / fh[:, None]).astype(np.float32),
        "old": (1.0 * n((I, M))).astype(np.float32),
        "fade": (np.random.uniform(0.3, 0.9, (I, 1))).astype(np.float32),
        "offs": striped(idx),
        "offs2": striped(idx2),
        "offs3": striped(idx3),
    }


def reference(keys_words, keys_scales, wk, notes, old, fade, offs, offs2, offs3):
    idx = unstriped(offs)
    idx2 = unstriped(offs2)
    idx3 = unstriped(offs3)
    keysu = unpack_weight(keys_words, keys_scales, "e2m1")
    wkq = mxq(f64(wk), 0, "e4m3")
    keysidxg = keysu[:, idx]
    kp = wkq.T @ keysidxg
    kpq = mxq(kp, 0, "e4m3")
    notesidx2q = mxq(f64(notes)[:, idx2], 0, "e4m3")
    g0 = kpq.T @ notesidx2q
    gf = np.zeros((I, M))
    gf[:, idx3] = g0
    y = f64(old) * f64(fade) + gf
    words, scales = planes(y)
    return y, words, scales

@@ -1,0 +1,217 @@
+from contextlib import ExitStack
+
+import concourse.mybir as mybir
+
+D, T, I, J, U, H, M = 512, 2048, 512, 512, 1024, 512, 1024
+FLOPS = 2 * D * H * I + 2 * H * I * J
+
+F32 = mybir.dt.float32
+BF16 = mybir.dt.bfloat16
+I32 = mybir.dt.int32
+U32 = mybir.dt.uint32
+U16 = mybir.dt.uint16
+U8 = mybir.dt.uint8
+FP8X4 = mybir.dt.float8_e4m3fn_x4
+FP4X4 = mybir.dt.float4_e2m1fn_x4
+COPY = mybir.ActivationFunctionType.Copy
+MULT = mybir.AluOpType.mult
+ADD = mybir.AluOpType.add
+
+P = 128
+PACK = 4
+HALF = J // 2
+WK_SPLIT = 48
+LAST_SPLIT = 384
+CHUNK = 256
+
+
+def tile_attend_tab_made_keep_pl_kernel(
+    tc, keys_words, keys_scales, wk, notes, old, fade, offs, offs2, offs3, out_0, out_1, out_2
+):
+    nc = tc.nc
+    with ExitStack() as ctx:
+        keep = ctx.enter_context(tc.tile_pool(name="keep", bufs=1))
+        psum = ctx.enter_context(tc.psum_pool(name="psum", bufs=1))
+
+        def quantize(codes, scales, values):
+            nc.vector.quantize_mx(out=codes.bitcast(FP8X4), scales=scales, in_=values)
+
+        def entries(offsets, first, last):
+            return offsets[:, first // 16 : last // 16]
+
+        pool_words = keep.tile([P, T], U16, name="pool_words")
+        pool_scales = keep.tile([P, T], U8, name="pool_scales")
+        key_list = keep.tile([P, I // 16], U16, name="key_list")
+        note_list = keep.tile([P, J // 16], U16, name="note_list")
+        place_list = keep.tile([P, J // 16], U16, name="place_list")
+        wk_rows = keep.tile([P, PACK, H], F32, name="wk_rows")
+        note_rows = [keep.tile([P, U], F32, name="note_rows%d" % t) for t in range(PACK)]
+        old_rows = [keep.tile([P, M], F32, name="old_rows%d" % r) for r in range(PACK)]
+        fade_cols = keep.tile([P, PACK], F32, name="fade_cols")
+        placed = [keep.tile([P, M], F32, name="placed%d" % r) for r in range(PACK)]
+
+        nc.vector.memset(pool_scales[:].bitcast(I32), 0)
+        nc.sync.dma_start(out=pool_words[:].bitcast(I32), in_=keys_words[0].bitcast(I32))
+        for q in range(4):
+            nc.sync.dma_start(
+                out=pool_scales[32 * q : 32 * q + 4, :].bitcast(I32),
+                in_=keys_scales[0, 4 * q : 4 * q + 4, :].bitcast(I32),
+            )
+        nc.sync.dma_start(out=key_list[:], in_=offs)
+        nc.sync.dma_start(out=wk_rows[:], in_=wk.rearrange("(p j) h -> p j h", j=PACK))
+        nc.sync.dma_start(out=note_list[:], in_=offs2)
+        notes_by_plane = notes.rearrange("(p t) u -> p t u", t=PACK)
+        for t in range(PACK):
+            nc.sync.dma_start(out=note_rows[t][:], in_=notes_by_plane[:, t, :])
+        nc.sync.dma_start(out=place_list[:], in_=offs3)
+        nc.sync.dma_start(out=fade_cols[:], in_=fade.rearrange("(p r) o -> p (r o)", r=PACK))
+        old_by_row = old.rearrange("(p r) m -> p r m", r=PACK)
+        for r in (1, 0, 2, 3):
+            nc.sync.dma_start(out=old_rows[r][:], in_=old_by_row[:, r, :])
+        for r in range(PACK):
+            (nc.gpsimd, nc.vector)[r % 2].memset(placed[r][:], 0.0)
+
+        key_words = keep.tile([P, I], U16, name="key_words", align_bytes=64)
+        key_scales = keep.tile([P, I], U8, name="key_scales", align_bytes=64)
+        nc.vector.tensor_copy(key_words[:], pool_words[:].indirect(key_list[:]))
+        nc.vector.tensor_copy(key_scales[:], pool_scales[:].indirect(key_list[:]))
+
+        wk_grouped = keep.tile([P, H * PACK], BF16, name="wk_grouped", align_bytes=64)
+        wk_dst = wk_grouped[:].rearrange("p (t m j) -> p m j t", t=PACK, j=PACK)
+        wk_src = wk_rows[:].rearrange("p j (m t) -> p m j t", t=PACK)
+        nc.scalar.copy(wk_dst[:, :WK_SPLIT], wk_src[:, :WK_SPLIT])
+        nc.vector.tensor_copy(wk_dst[:, WK_SPLIT:], wk_src[:, WK_SPLIT:])
+        wk_codes = keep.tile([P, H], U32, name="wk_codes", align_bytes=64)
+        wk_scales = keep.tile([P, H], U8, name="wk_scales", align_bytes=64)
+        quantize(wk_codes[:], wk_scales[:], wk_grouped[:])
+
+        note_picked = keep.tile([P, PACK, J], BF16, name="note_picked")
+        for t in range(PACK):
+            nc.scalar.activation(note_picked[:, t, :], note_rows[t][:].indirect(note_list[:]), COPY)
+
+        kp_grouped = keep.tile([P, I * PACK], BF16, name="kp_grouped", align_bytes=64)
+        kp_dst = kp_grouped[:].rearrange("p (r s t) -> p r s t", r=PACK, t=PACK)
+        for b in range(PACK):
+            bank = psum.tile([P, PACK, P], F32, name="kp_bank%d" % b, tag="low%d" % b)
+            cols = slice(b * P, (b + 1) * P)
+            for t in range(PACK):
+                nc.tensor.matmul_mx(
+                    out=bank[:, t, :],
+                    lhsT=wk_codes[:, t * P : (t + 1) * P].bitcast(FP8X4),
+                    lhsT_scale=wk_scales[:, t * P : (t + 1) * P],
+                    rhs=key_words[:, cols].bitcast(FP4X4),
+                    rhs_scale=key_scales[:, cols],
+                    start=True,
+                    stop=True,
+                )
+            nc.vector.tensor_copy(
+                kp_dst[:, :, 32 * b : 32 * (b + 1), :],
+                bank[:].rearrange("p t (s r) -> p r s t", r=PACK),
+            )
+        kp_codes = keep.tile([P, I], U32, name="kp_codes", align_bytes=64)
+        kp_scales = keep.tile([P, I], U8, name="kp_scales", align_bytes=64)
+        quantize(kp_codes[:], kp_scales[:], kp_grouped[:])
+
+        note_codes, note_scales = [], []
+        note_grouped = []
+        for half, copy in enumerate((nc.vector.tensor_copy, nc.scalar.copy)):
+            grouped = keep.tile([P, HALF, PACK], BF16, name="note_grouped%d" % half, align_bytes=64)
+            copy(
+                grouped[:].rearrange("p (c i) t -> p c t i", i=4),
+                note_picked[:, :, half * HALF : (half + 1) * HALF].rearrange("p t (c i) -> p c t i", i=4),
+            )
+            note_grouped.append(grouped)
+        for half in range(2):
+            codes = keep.tile([P, HALF], U32, name="note_codes%d" % half, align_bytes=64)
+            scales = keep.tile([P, HALF], U8, name="note_scales%d" % half, align_bytes=64)
+            quantize(codes[:], scales[:], note_grouped[half][:].rearrange("p j t -> p (j t)"))
+            note_codes.append(codes)
+            note_scales.append(scales)
+
+        table_banks = {}
+        for half in range(2):
+            for r in range(PACK):
+                tag = ("high%d", "low%d")[half] % r
+                bank = psum.tile([P, PACK, P], F32, name="g0_bank%d_%d" % (r, half), tag=tag)
+                acc = bank[:].rearrange("p a b -> p (a b)")[:, :HALF]
+                nc.tensor.matmul_mx(
+                    out=acc,
+                    lhsT=kp_codes[:, r * P : (r + 1) * P].bitcast(FP8X4),
+                    lhsT_scale=kp_scales[:, r * P : (r + 1) * P],
+                    rhs=note_codes[half][:].bitcast(FP8X4),
+                    rhs_scale=note_scales[half][:],
+                    start=True,
+                    stop=True,
+                )
+                table_banks[r, half] = acc
+
+        table = [keep.tile([P, J], F32, name="table%d" % r) for r in range(PACK)]
+        result = keep.tile([P, PACK, M], F32, name="result")
+        out_rows = out_0.rearrange("(p r) m -> p r m", r=PACK)
+
+        def fetch(copy, r, half):
+            copy(table[r][:, half * HALF : (half + 1) * HALF], table_banks[r, half])
+
+        def scatter_scalar(r, first, last):
+            nc.scalar.activation(
+                placed[r][:].indirect(entries(place_list, first, last)), table[r][:, first:last], COPY
+            )
+
+        def scatter_vector(r, first, last):
+            nc.vector.tensor_copy(
+                placed[r][:].indirect(entries(place_list, first, last)), table[r][:, first:last]
+            )
+
+        def combine(r, cols):
+            nc.vector.scalar_tensor_tensor(
+                result[:, r, cols], old_rows[r][:, cols], fade_cols[:, r : r + 1], placed[r][:, cols], MULT, ADD
+            )
+
+        def store(r):
+            nc.sync.dma_start(out=out_rows[:, r, :], in_=result[:, r, :])
+
+        everything = slice(0, M)
+        for half in range(2):
+            fetch(nc.scalar.copy, 0, half)
+            scatter_scalar(0, half * HALF, (half + 1) * HALF)
+            fetch(nc.vector.tensor_copy, 1, half)
+            scatter_vector(1, half * HALF, (half + 1) * HALF)
+        for r in (3, 2):
+            for half in range(2):
+                fetch(nc.scalar.copy, r, half)
+        for r in (1, 0):
+            combine(r, everything)
+            store(r)
+        for half in range(2):
+            scatter_scalar(2, half * HALF, (half + 1) * HALF)
+        scatter_vector(3, 0, LAST_SPLIT)
+        scatter_scalar(3, LAST_SPLIT, J)
+        combine(2, everything)
+        store(2)
+
+        chunks = M // CHUNK
+        for c in range(chunks):
+            combine(3, slice(c * CHUNK, (c + 1) * CHUNK))
+        store(3)
+
+        plane_scales = keep.tile([P, M], U8, name="plane_scales", align_bytes=64)
+        words_out = out_1[0].rearrange("p m r -> p (m r)").bitcast(I32)
+        grouped_chunks = {}
+        for c, copy in ((0, nc.scalar.copy), (2, nc.vector.tensor_copy), (1, nc.scalar.copy), (3, nc.vector.tensor_copy)):
+            grouped = keep.tile([P, CHUNK, PACK], BF16, name="result_grouped%d" % c, align_bytes=64)
+            copy(
+                grouped[:].rearrange("p (c i) r -> p c r i", i=4),
+                result[:, :, c * CHUNK : (c + 1) * CHUNK].rearrange("p r (c i) -> p c r i", i=4),
+            )
+            grouped_chunks[c] = grouped
+        for c in (0, 2, 3, 1):
+            cols = slice(c * CHUNK, (c + 1) * CHUNK)
+            codes = keep.tile([P, CHUNK], U32, name="plane_codes%d" % c, align_bytes=64)
+            quantize(codes[:], plane_scales[:, cols], grouped_chunks[c][:].rearrange("p m r -> p (m r)"))
+            nc.sync.dma_start(out=words_out[:, cols], in_=codes[:].bitcast(I32))
+        for q in range(4):
+            queue = (nc.scalar, nc.sync)[q % 2]
+            queue.dma_start(
+                out=out_2[0, 4 * q : 4 * q + 4, :].bitcast(I32),
+                in_=plane_scales[32 * q : 32 * q + 4, :].bitcast(I32),
+            )

@@ -20,7 +20,6 @@ ADD = mybir.AluOpType.add
 P = 128
 PACK = 4
 HALF = J // 2
-WK_SPLIT = 48
 LAST_SPLIT = 384
 CHUNK = 256
 
@@ -44,21 +43,24 @@ def tile_attend_tab_made_keep_pl_kernel(
         key_list = keep.tile([P, I // 16], U16, name="key_list")
         note_list = keep.tile([P, J // 16], U16, name="note_list")
         place_list = keep.tile([P, J // 16], U16, name="place_list")
-        wk_rows = keep.tile([P, PACK, H], F32, name="wk_rows")
+        wk_rows = [keep.tile([P, PACK, H // 2], F32, name="wk_rows%d" % half) for half in range(2)]
         note_rows = [keep.tile([P, U], F32, name="note_rows%d" % t) for t in range(PACK)]
         old_rows = [keep.tile([P, M], F32, name="old_rows%d" % r) for r in range(PACK)]
         fade_cols = keep.tile([P, PACK], F32, name="fade_cols")
-        placed = [keep.tile([P, M], F32, name="placed%d" % r) for r in range(PACK)]
+        windows = [keep.tile([P, M], F32, name="window%d" % w) for w in range(3)]
+        placed = [windows[0], windows[1], windows[2], windows[1]]
 
         nc.vector.memset(pool_scales[:].bitcast(I32), 0)
+        nc.sync.dma_start(out=key_list[:], in_=offs)
         nc.sync.dma_start(out=pool_words[:].bitcast(I32), in_=keys_words[0].bitcast(I32))
         for q in range(4):
             nc.sync.dma_start(
-                out=pool_scales[32 * q : 32 * q + 4, :].bitcast(I32),
-                in_=keys_scales[0, 4 * q : 4 * q + 4, :].bitcast(I32),
+                out=pool_scales[q:P:32, :].bitcast(I32),
+                in_=keys_scales[0, q:16:4, :].bitcast(I32),
             )
-        nc.sync.dma_start(out=key_list[:], in_=offs)
-        nc.sync.dma_start(out=wk_rows[:], in_=wk.rearrange("(p j) h -> p j h", j=PACK))
+        wk_by_row = wk.rearrange("(p j) h -> p j h", j=PACK)
+        for half in range(2):
+            nc.sync.dma_start(out=wk_rows[half][:], in_=wk_by_row[:, :, half * (H // 2) : (half + 1) * (H // 2)])
         nc.sync.dma_start(out=note_list[:], in_=offs2)
         notes_by_plane = notes.rearrange("(p t) u -> p t u", t=PACK)
         for t in range(PACK):
@@ -66,10 +68,10 @@ def tile_attend_tab_made_keep_pl_kernel(
         nc.sync.dma_start(out=place_list[:], in_=offs3)
         nc.sync.dma_start(out=fade_cols[:], in_=fade.rearrange("(p r) o -> p (r o)", r=PACK))
         old_by_row = old.rearrange("(p r) m -> p r m", r=PACK)
-        for r in (1, 0, 2, 3):
-            nc.sync.dma_start(out=old_rows[r][:], in_=old_by_row[:, r, :])
         for r in range(PACK):
-            (nc.gpsimd, nc.vector)[r % 2].memset(placed[r][:], 0.0)
+            nc.sync.dma_start(out=old_rows[r][:], in_=old_by_row[:, r, :])
+        for window in windows:
+            nc.vector.memset(window[:], 0.0)
 
         key_words = keep.tile([P, I], U16, name="key_words", align_bytes=64)
         key_scales = keep.tile([P, I], U8, name="key_scales", align_bytes=64)
@@ -78,16 +80,27 @@ def tile_attend_tab_made_keep_pl_kernel(
 
         wk_grouped = keep.tile([P, H * PACK], BF16, name="wk_grouped", align_bytes=64)
         wk_dst = wk_grouped[:].rearrange("p (t m j) -> p m j t", t=PACK, j=PACK)
-        wk_src = wk_rows[:].rearrange("p j (m t) -> p m j t", t=PACK)
-        nc.scalar.copy(wk_dst[:, :WK_SPLIT], wk_src[:, :WK_SPLIT])
-        nc.vector.tensor_copy(wk_dst[:, WK_SPLIT:], wk_src[:, WK_SPLIT:])
+        for half, copy in enumerate((nc.scalar.copy, nc.vector.tensor_copy)):
+            copy(
+                wk_dst[:, half * (P // 2) : (half + 1) * (P // 2)],
+                wk_rows[half][:].rearrange("p j (m t) -> p m j t", t=PACK),
+            )
         wk_codes = keep.tile([P, H], U32, name="wk_codes", align_bytes=64)
         wk_scales = keep.tile([P, H], U8, name="wk_scales", align_bytes=64)
-        quantize(wk_codes[:], wk_scales[:], wk_grouped[:])
+        for t in range(PACK):
+            cols = slice(t * P, (t + 1) * P)
+            quantize(wk_codes[:, cols], wk_scales[:, cols], wk_grouped[:, t * H : (t + 1) * H])
 
         note_picked = keep.tile([P, PACK, J], BF16, name="note_picked")
-        for t in range(PACK):
+        for t in range(PACK - 1):
             nc.scalar.activation(note_picked[:, t, :], note_rows[t][:].indirect(note_list[:]), COPY)
+        for half in range(2):
+            first, last = half * HALF, (half + 1) * HALF
+            nc.scalar.activation(
+                note_picked[:, PACK - 1, first:last],
+                note_rows[PACK - 1][:].indirect(entries(note_list, first, last)),
+                COPY,
+            )
 
         kp_grouped = keep.tile([P, I * PACK], BF16, name="kp_grouped", align_bytes=64)
         kp_dst = kp_grouped[:].rearrange("p (r s t) -> p r s t", r=PACK, t=PACK)
@@ -110,9 +123,11 @@ def tile_attend_tab_made_keep_pl_kernel(
             )
         kp_codes = keep.tile([P, I], U32, name="kp_codes", align_bytes=64)
         kp_scales = keep.tile([P, I], U8, name="kp_scales", align_bytes=64)
-        quantize(kp_codes[:], kp_scales[:], kp_grouped[:])
 
-        note_codes, note_scales = [], []
+        def quantize_keys(first, last):
+            cols = slice(first * P, last * P)
+            quantize(kp_codes[:, cols], kp_scales[:, cols], kp_grouped[:, first * I : last * I])
+
         note_grouped = []
         for half, copy in enumerate((nc.vector.tensor_copy, nc.scalar.copy)):
             grouped = keep.tile([P, HALF, PACK], BF16, name="note_grouped%d" % half, align_bytes=64)
@@ -121,36 +136,36 @@ def tile_attend_tab_made_keep_pl_kernel(
                 note_picked[:, :, half * HALF : (half + 1) * HALF].rearrange("p t (c i) -> p c t i", i=4),
             )
             note_grouped.append(grouped)
+        note_codes = keep.tile([P, J], U32, name="note_codes", align_bytes=64)
+        note_scales = keep.tile([P, J], U8, name="note_scales", align_bytes=64)
         for half in range(2):
-            codes = keep.tile([P, HALF], U32, name="note_codes%d" % half, align_bytes=64)
-            scales = keep.tile([P, HALF], U8, name="note_scales%d" % half, align_bytes=64)
-            quantize(codes[:], scales[:], note_grouped[half][:].rearrange("p j t -> p (j t)"))
-            note_codes.append(codes)
-            note_scales.append(scales)
+            quantize_keys(2 * half, 2 * half + 2)
+            cols = slice(half * HALF, (half + 1) * HALF)
+            quantize(note_codes[:, cols], note_scales[:, cols], note_grouped[half][:].rearrange("p j t -> p (j t)"))
 
+        pieces = [(0, 0, HALF), (1, 0, HALF), (0, HALF, J), (1, HALF, J), (3, 0, J), (2, 0, J)]
+        tags = ["high0", "high1", "high2", "high3", "low0", "low1"]
         table_banks = {}
-        for half in range(2):
-            for r in range(PACK):
-                tag = ("high%d", "low%d")[half] % r
-                bank = psum.tile([P, PACK, P], F32, name="g0_bank%d_%d" % (r, half), tag=tag)
-                acc = bank[:].rearrange("p a b -> p (a b)")[:, :HALF]
-                nc.tensor.matmul_mx(
-                    out=acc,
-                    lhsT=kp_codes[:, r * P : (r + 1) * P].bitcast(FP8X4),
-                    lhsT_scale=kp_scales[:, r * P : (r + 1) * P],
-                    rhs=note_codes[half][:].bitcast(FP8X4),
-                    rhs_scale=note_scales[half][:],
-                    start=True,
-                    stop=True,
-                )
-                table_banks[r, half] = acc
+        for (r, first, last), tag in zip(pieces, tags):
+            bank = psum.tile([P, PACK, P], F32, name="g0_bank%d_%d" % (r, first), tag=tag)
+            acc = bank[:].rearrange("p a b -> p (a b)")[:, : last - first]
+            nc.tensor.matmul_mx(
+                out=acc,
+                lhsT=kp_codes[:, r * P : (r + 1) * P].bitcast(FP8X4),
+                lhsT_scale=kp_scales[:, r * P : (r + 1) * P],
+                rhs=note_codes[:, first:last].bitcast(FP8X4),
+                rhs_scale=note_scales[:, first:last],
+                start=True,
+                stop=True,
+            )
+            table_banks[r, first, last] = acc
 
         table = [keep.tile([P, J], F32, name="table%d" % r) for r in range(PACK)]
         result = keep.tile([P, PACK, M], F32, name="result")
         out_rows = out_0.rearrange("(p r) m -> p r m", r=PACK)
 
-        def fetch(copy, r, half):
-            copy(table[r][:, half * HALF : (half + 1) * HALF], table_banks[r, half])
+        def fetch(copy, r, first, last):
+            copy(table[r][:, first:last], table_banks[r, first, last])
 
         def scatter_scalar(r, first, last):
             nc.scalar.activation(
@@ -172,27 +187,26 @@ def tile_attend_tab_made_keep_pl_kernel(
 
         everything = slice(0, M)
         for half in range(2):
-            fetch(nc.scalar.copy, 0, half)
-            scatter_scalar(0, half * HALF, (half + 1) * HALF)
-            fetch(nc.vector.tensor_copy, 1, half)
-            scatter_vector(1, half * HALF, (half + 1) * HALF)
+            first, last = half * HALF, (half + 1) * HALF
+            fetch(nc.scalar.copy, 0, first, last)
+            scatter_scalar(0, first, last)
+            fetch(nc.vector.tensor_copy, 1, first, last)
+            scatter_vector(1, first, last)
         for r in (3, 2):
-            for half in range(2):
-                fetch(nc.scalar.copy, r, half)
-        for r in (1, 0):
+            fetch(nc.scalar.copy, r, 0, J)
+        for r in (0, 1):
             combine(r, everything)
             store(r)
         for half in range(2):
             scatter_scalar(2, half * HALF, (half + 1) * HALF)
-        scatter_vector(3, 0, LAST_SPLIT)
-        scatter_scalar(3, LAST_SPLIT, J)
-        combine(2, everything)
-        store(2)
+        scatter_vector(3, 0, J)
+        combine(3, everything)
+        store(3)
 
         chunks = M // CHUNK
         for c in range(chunks):
-            combine(3, slice(c * CHUNK, (c + 1) * CHUNK))
-        store(3)
+            combine(2, slice(c * CHUNK, (c + 1) * CHUNK))
+        store(2)
 
         plane_scales = keep.tile([P, M], U8, name="plane_scales", align_bytes=64)
         words_out = out_1[0].rearrange("p m r -> p (m r)").bitcast(I32)
@@ -212,6 +226,6 @@ def tile_attend_tab_made_keep_pl_kernel(
         for q in range(4):
             queue = (nc.scalar, nc.sync)[q % 2]
             queue.dma_start(
-                out=out_2[0, 4 * q : 4 * q + 4, :].bitcast(I32),
-                in_=plane_scales[32 * q : 32 * q + 4, :].bitcast(I32),
+                out=out_2[0, q:16:4, :].bitcast(I32),
+                in_=plane_scales[q:P:32, :].bitcast(I32),
             )

from contextlib import ExitStack

import concourse.mybir as mybir

D, T, I, J, U, H, M = 512, 2048, 512, 512, 1024, 512, 1024
FLOPS = 2 * D * H * I + 2 * H * I * J

F32 = mybir.dt.float32
BF16 = mybir.dt.bfloat16
I32 = mybir.dt.int32
U32 = mybir.dt.uint32
U16 = mybir.dt.uint16
U8 = mybir.dt.uint8
FP8X4 = mybir.dt.float8_e4m3fn_x4
FP4X4 = mybir.dt.float4_e2m1fn_x4
COPY = mybir.ActivationFunctionType.Copy
MULT = mybir.AluOpType.mult
ADD = mybir.AluOpType.add

P = 128
PACK = 4
HALF = J // 2
LAST_SPLIT = 384
CHUNK = 256


def tile_attend_tab_made_keep_pl_kernel(
    tc, keys_words, keys_scales, wk, notes, old, fade, offs, offs2, offs3, out_0, out_1, out_2
):
    nc = tc.nc
    with ExitStack() as ctx:
        keep = ctx.enter_context(tc.tile_pool(name="keep", bufs=1))
        psum = ctx.enter_context(tc.psum_pool(name="psum", bufs=1))

        def quantize(codes, scales, values):
            nc.vector.quantize_mx(out=codes.bitcast(FP8X4), scales=scales, in_=values)

        def entries(offsets, first, last):
            return offsets[:, first // 16 : last // 16]

        pool_words = keep.tile([P, T], U16, name="pool_words")
        pool_scales = keep.tile([P, T], U8, name="pool_scales")
        key_list = keep.tile([P, I // 16], U16, name="key_list")
        note_list = keep.tile([P, J // 16], U16, name="note_list")
        place_list = keep.tile([P, J // 16], U16, name="place_list")
        wk_rows = [keep.tile([P, PACK, H // 2], F32, name="wk_rows%d" % half) for half in range(2)]
        note_rows = [keep.tile([P, U], F32, name="note_rows%d" % t) for t in range(PACK)]
        old_rows = [keep.tile([P, M], F32, name="old_rows%d" % r) for r in range(PACK)]
        fade_cols = keep.tile([P, PACK], F32, name="fade_cols")
        windows = [keep.tile([P, M], F32, name="window%d" % w) for w in range(3)]
        placed = [windows[0], windows[1], windows[2], windows[1]]

        nc.vector.memset(pool_scales[:].bitcast(I32), 0)
        nc.sync.dma_start(out=key_list[:], in_=offs)
        nc.sync.dma_start(out=pool_words[:].bitcast(I32), in_=keys_words[0].bitcast(I32))
        for q in range(4):
            nc.sync.dma_start(
                out=pool_scales[q:P:32, :].bitcast(I32),
                in_=keys_scales[0, q:16:4, :].bitcast(I32),
            )
        wk_by_row = wk.rearrange("(p j) h -> p j h", j=PACK)
        for half in range(2):
            nc.sync.dma_start(out=wk_rows[half][:], in_=wk_by_row[:, :, half * (H // 2) : (half + 1) * (H // 2)])
        nc.sync.dma_start(out=note_list[:], in_=offs2)
        notes_by_plane = notes.rearrange("(p t) u -> p t u", t=PACK)
        for t in range(PACK):
            nc.sync.dma_start(out=note_rows[t][:], in_=notes_by_plane[:, t, :])
        nc.sync.dma_start(out=place_list[:], in_=offs3)
        nc.sync.dma_start(out=fade_cols[:], in_=fade.rearrange("(p r) o -> p (r o)", r=PACK))
        old_by_row = old.rearrange("(p r) m -> p r m", r=PACK)
        for r in range(PACK):
            nc.sync.dma_start(out=old_rows[r][:], in_=old_by_row[:, r, :])
        for window in windows:
            nc.vector.memset(window[:], 0.0)

        key_words = keep.tile([P, I], U16, name="key_words", align_bytes=64)
        key_scales = keep.tile([P, I], U8, name="key_scales", align_bytes=64)
        nc.vector.tensor_copy(key_words[:], pool_words[:].indirect(key_list[:]))
        nc.vector.tensor_copy(key_scales[:], pool_scales[:].indirect(key_list[:]))

        wk_grouped = keep.tile([P, H * PACK], BF16, name="wk_grouped", align_bytes=64)
        wk_dst = wk_grouped[:].rearrange("p (t m j) -> p m j t", t=PACK, j=PACK)
        for half, copy in enumerate((nc.scalar.copy, nc.vector.tensor_copy)):
            copy(
                wk_dst[:, half * (P // 2) : (half + 1) * (P // 2)],
                wk_rows[half][:].rearrange("p j (m t) -> p m j t", t=PACK),
            )
        wk_codes = keep.tile([P, H], U32, name="wk_codes", align_bytes=64)
        wk_scales = keep.tile([P, H], U8, name="wk_scales", align_bytes=64)
        for t in range(PACK):
            cols = slice(t * P, (t + 1) * P)
            quantize(wk_codes[:, cols], wk_scales[:, cols], wk_grouped[:, t * H : (t + 1) * H])

        note_picked = keep.tile([P, PACK, J], BF16, name="note_picked")
        for t in range(PACK - 1):
            nc.scalar.activation(note_picked[:, t, :], note_rows[t][:].indirect(note_list[:]), COPY)
        for half in range(2):
            first, last = half * HALF, (half + 1) * HALF
            nc.scalar.activation(
                note_picked[:, PACK - 1, first:last],
                note_rows[PACK - 1][:].indirect(entries(note_list, first, last)),
                COPY,
            )

        kp_grouped = keep.tile([P, I * PACK], BF16, name="kp_grouped", align_bytes=64)
        kp_dst = kp_grouped[:].rearrange("p (r s t) -> p r s t", r=PACK, t=PACK)
        for b in range(PACK):
            bank = psum.tile([P, PACK, P], F32, name="kp_bank%d" % b, tag="low%d" % b)
            cols = slice(b * P, (b + 1) * P)
            for t in range(PACK):
                nc.tensor.matmul_mx(
                    out=bank[:, t, :],
                    lhsT=wk_codes[:, t * P : (t + 1) * P].bitcast(FP8X4),
                    lhsT_scale=wk_scales[:, t * P : (t + 1) * P],
                    rhs=key_words[:, cols].bitcast(FP4X4),
                    rhs_scale=key_scales[:, cols],
                    start=True,
                    stop=True,
                )
            nc.vector.tensor_copy(
                kp_dst[:, :, 32 * b : 32 * (b + 1), :],
                bank[:].rearrange("p t (s r) -> p r s t", r=PACK),
            )
        kp_codes = keep.tile([P, I], U32, name="kp_codes", align_bytes=64)
        kp_scales = keep.tile([P, I], U8, name="kp_scales", align_bytes=64)

        def quantize_keys(first, last):
            cols = slice(first * P, last * P)
            quantize(kp_codes[:, cols], kp_scales[:, cols], kp_grouped[:, first * I : last * I])

        note_grouped = []
        for half, copy in enumerate((nc.vector.tensor_copy, nc.scalar.copy)):
            grouped = keep.tile([P, HALF, PACK], BF16, name="note_grouped%d" % half, align_bytes=64)
            copy(
                grouped[:].rearrange("p (c i) t -> p c t i", i=4),
                note_picked[:, :, half * HALF : (half + 1) * HALF].rearrange("p t (c i) -> p c t i", i=4),
            )
            note_grouped.append(grouped)
        note_codes = keep.tile([P, J], U32, name="note_codes", align_bytes=64)
        note_scales = keep.tile([P, J], U8, name="note_scales", align_bytes=64)
        for half in range(2):
            quantize_keys(2 * half, 2 * half + 2)
            cols = slice(half * HALF, (half + 1) * HALF)
            quantize(note_codes[:, cols], note_scales[:, cols], note_grouped[half][:].rearrange("p j t -> p (j t)"))

        pieces = [(0, 0, HALF), (1, 0, HALF), (0, HALF, J), (1, HALF, J), (3, 0, J), (2, 0, J)]
        tags = ["high0", "high1", "high2", "high3", "low0", "low1"]
        table_banks = {}
        for (r, first, last), tag in zip(pieces, tags):
            bank = psum.tile([P, PACK, P], F32, name="g0_bank%d_%d" % (r, first), tag=tag)
            acc = bank[:].rearrange("p a b -> p (a b)")[:, : last - first]
            nc.tensor.matmul_mx(
                out=acc,
                lhsT=kp_codes[:, r * P : (r + 1) * P].bitcast(FP8X4),
                lhsT_scale=kp_scales[:, r * P : (r + 1) * P],
                rhs=note_codes[:, first:last].bitcast(FP8X4),
                rhs_scale=note_scales[:, first:last],
                start=True,
                stop=True,
            )
            table_banks[r, first, last] = acc

        table = [keep.tile([P, J], F32, name="table%d" % r) for r in range(PACK)]
        result = keep.tile([P, PACK, M], F32, name="result")
        out_rows = out_0.rearrange("(p r) m -> p r m", r=PACK)

        def fetch(copy, r, first, last):
            copy(table[r][:, first:last], table_banks[r, first, last])

        def scatter_scalar(r, first, last):
            nc.scalar.activation(
                placed[r][:].indirect(entries(place_list, first, last)), table[r][:, first:last], COPY
            )

        def scatter_vector(r, first, last):
            nc.vector.tensor_copy(
                placed[r][:].indirect(entries(place_list, first, last)), table[r][:, first:last]
            )

        def combine(r, cols):
            nc.vector.scalar_tensor_tensor(
                result[:, r, cols], old_rows[r][:, cols], fade_cols[:, r : r + 1], placed[r][:, cols], MULT, ADD
            )

        def store(r):
            nc.sync.dma_start(out=out_rows[:, r, :], in_=result[:, r, :])

        everything = slice(0, M)
        for half in range(2):
            first, last = half * HALF, (half + 1) * HALF
            fetch(nc.scalar.copy, 0, first, last)
            scatter_scalar(0, first, last)
            fetch(nc.vector.tensor_copy, 1, first, last)
            scatter_vector(1, first, last)
        for r in (3, 2):
            fetch(nc.scalar.copy, r, 0, J)
        for r in (0, 1):
            combine(r, everything)
            store(r)
        for half in range(2):
            scatter_scalar(2, half * HALF, (half + 1) * HALF)
        scatter_vector(3, 0, J)
        combine(3, everything)
        store(3)

        chunks = M // CHUNK
        for c in range(chunks):
            combine(2, slice(c * CHUNK, (c + 1) * CHUNK))
        store(2)

        plane_scales = keep.tile([P, M], U8, name="plane_scales", align_bytes=64)
        words_out = out_1[0].rearrange("p m r -> p (m r)").bitcast(I32)
        grouped_chunks = {}
        for c, copy in ((0, nc.scalar.copy), (2, nc.vector.tensor_copy), (1, nc.scalar.copy), (3, nc.vector.tensor_copy)):
            grouped = keep.tile([P, CHUNK, PACK], BF16, name="result_grouped%d" % c, align_bytes=64)
            copy(
                grouped[:].rearrange("p (c i) r -> p c r i", i=4),
                result[:, :, c * CHUNK : (c + 1) * CHUNK].rearrange("p r (c i) -> p c r i", i=4),
            )
            grouped_chunks[c] = grouped
        for c in (0, 2, 3, 1):
            cols = slice(c * CHUNK, (c + 1) * CHUNK)
            codes = keep.tile([P, CHUNK], U32, name="plane_codes%d" % c, align_bytes=64)
            quantize(codes[:], plane_scales[:, cols], grouped_chunks[c][:].rearrange("p m r -> p (m r)"))
            nc.sync.dma_start(out=words_out[:, cols], in_=codes[:].bitcast(I32))
        for q in range(4):
            queue = (nc.scalar, nc.sync)[q % 2]
            queue.dma_start(
                out=out_2[0, q:16:4, :].bitcast(I32),
                in_=plane_scales[q:P:32, :].bitcast(I32),
            )
